import numpy as np
import ml_dtypes


def mxq(x, axis, fmt="e4m3"):
    dtype, down = {"e4m3": (ml_dtypes.float8_e4m3fn, 7), "e5m2": (ml_dtypes.float8_e5m2, 14)}[fmt]
    v = np.moveaxis(np.asarray(x, np.float32).astype(ml_dtypes.bfloat16).astype(np.float64), axis, -1)
    blocks = v.reshape(v.shape[:-1] + (-1, 32))
    amax = np.abs(blocks).max(-1, keepdims=True)
    byte = np.maximum(np.where(amax > 0, np.frexp(amax)[1] - 1 + 127, 0) - down, 1)
    scale = np.exp2(byte - 127.0)
    codes = (blocks / scale).astype(np.float32).astype(dtype).astype(np.float64)
    return np.moveaxis((codes * scale).reshape(v.shape), -1, axis)


WIDE = False


def mx_kscale(k):
    if not WIDE:
        return np.ones(k)
    levels = np.array([30, -30])
    if k % 512:
        return np.exp2(np.random.permutation(np.resize(levels, k // 32))).repeat(32)
    a = np.empty((k // 512, 16))
    for p in range(k // 512):
        a[p, :8] = np.random.permutation(np.resize(levels, 8))
        for g in range(8):
            far = levels[np.abs(levels - a[p, g]) >= 10]
            a[p, g + 8] = far[np.random.randint(len(far))]
    return np.exp2(a.ravel()).repeat(32)


def f64(x):
    return np.asarray(x).astype(np.float64)


def striped(idx):
    return np.tile(np.asarray(idx).reshape(-1, 16).T, (8, 1)).astype(np.uint16)


def unstriped(offs):
    return offs[:16].T.reshape(-1).astype(np.int64)


K, J, N, T, V, E = 256, 1024, 256, 2048, 2048, 128


def setup_inputs():
    n = np.random.standard_normal
    idx = np.random.permutation(T)[:J]
    idx2 = np.random.permutation(V)[:J]
    idx3 = np.random.permutation(N)[:E]
    fj = mx_kscale(J)
    return {
        "xf": (n((K, T))).astype(np.float32),
        "ra": (np.random.uniform(0.5, 1.5, (1, J)) * fj).astype(np.float32),
        "gt": (n((N, V)) * np.exp(0.5 * n((1, V)))).astype(np.float32),
        "rb": (np.random.uniform(0.5, 1.5, (1, J)) / fj).astype(np.float32),
        "cp": (np.random.uniform(0.4, 1.2, (N, 1))).astype(np.float32),
        "old": (0.5 * n((K, E))).astype(np.float32),
        "offs": striped(idx),
        "offs2": striped(idx2),
        "offs3": striped(idx3),
    }


def reference(xf, ra, gt, rb, cp, old, offs, offs2, offs3):
    idx = unstriped(offs)
    idx2 = unstriped(offs2)
    idx3 = unstriped(offs3)
    xg = f64(xf)[:, idx]
    x1 = np.pad(xg, ((0, 0), (1, 0)))[:, :J]
    us = (xg - 0.6 * x1) * f64(ra)
    uj = us.T
    gs = np.minimum(f64(gt)[:, idx2], f64(cp)) * f64(rb)
    gj = gs.T
    ujq = mxq(uj, 0, "e5m2")
    gjq = mxq(gj, 0, "e5m2")
    w = ujq.T @ gjq
    y = 0.04 * w[:, idx3] + f64(old)
    return y

@@ -1,0 +1,206 @@
+from contextlib import ExitStack
+
+import concourse.mybir as mybir
+from concourse.masks import make_identity
+
+K, J, N, T, V, E = 256, 1024, 256, 2048, 2048, 128
+FLOPS = 2 * J * K * N
+
+F32 = mybir.dt.float32
+BF16 = mybir.dt.bfloat16
+U32 = mybir.dt.uint32
+U16 = mybir.dt.uint16
+U8 = mybir.dt.uint8
+E5M2X4 = mybir.dt.float8_e5m2_x4
+MULT = mybir.AluOpType.mult
+ADD = mybir.AluOpType.add
+MIN = mybir.AluOpType.min
+COPY = mybir.ActivationFunctionType.Copy
+
+P = 128
+PACK = 4
+J_PASS = P * PACK
+PASSES = J // J_PASS
+PIECE = 256
+PAD = 8
+
+
+def tile_list_moment_steps_bounded_columns_kernel(tc, xf, ra, gt, rb, cp, old, offs, offs2, offs3, out):
+    nc = tc.nc
+    with ExitStack() as ctx:
+        lists = ctx.enter_context(tc.tile_pool(name="lists", bufs=1))
+        keep = ctx.enter_context(tc.tile_pool(name="keep", bufs=1))
+        psum = ctx.enter_context(tc.psum_pool(name="psum", bufs=1))
+
+        list_x = lists.tile([P, J // 16], U16, name="list_x")
+        list_g = lists.tile([P, J // 16], U16, name="list_g")
+        list_w = lists.tile([P, E // 16], U16, name="list_w")
+        x_table = [keep.tile([P, T], F32, name="x_table%d" % h) for h in range(2)]
+        g_table = [keep.tile([P, V], F32, name="g_table%d" % h) for h in range(2)]
+        ra_sb = keep.tile([P, PASSES, PACK], F32, name="ra_sb")
+        rb_sb = keep.tile([P, PASSES, PACK], F32, name="rb_sb")
+        cp_sb = keep.tile([P, 2], F32, name="cp_sb")
+        old_sb = keep.tile([P, 2, E], F32, name="old_sb")
+        ident = keep.tile([P, P], F32, name="ident")
+
+        zero = keep.tile([P, 1], F32, name="zero")
+        nc.vector.memset(zero[:], 0.0)
+        make_identity(nc, ident[:])
+        nc.sync.dma_start(list_x[:], offs)
+        nc.scalar.dma_start(ra_sb[:], ra[0, :].rearrange("(a q t) -> q a t", a=PASSES, t=PACK))
+        nc.sync.dma_start(x_table[0][:], xf[0:P, :])
+        nc.scalar.dma_start(rb_sb[:], rb[0, :].rearrange("(a q t) -> q a t", a=PASSES, t=PACK))
+        with nc.allow_non_contiguous_dma(reason="one bound a partition"):
+            nc.scalar.dma_start(cp_sb[:], cp.rearrange("(h p) o -> p (h o)", p=P))
+        nc.sync.dma_start(x_table[1][:], xf[P : 2 * P, :])
+        nc.sync.dma_start(list_g[:], offs2)
+        nc.sync.dma_start(g_table[0][:], gt[0:P, :])
+        nc.sync.dma_start(g_table[1][:], gt[P : 2 * P, :])
+        nc.sync.dma_start(list_w[:], offs3)
+        nc.sync.dma_start(old_sb[:], old.rearrange("(h p) e -> p h e", p=P))
+
+        x_picked = [keep.tile([P, PAD + J], F32, name="x_picked%d" % h) for h in range(2)]
+        for h in range(2):
+            nc.scalar.activation(x_picked[h][:, PAD - 1 : PAD], zero[:], COPY)
+
+        rb_rows = [psum.tile([P, PACK, P], F32, name="rb_rows%d" % a, tag="bank%d" % a) for a in range(PASSES)]
+        for a in range(PASSES):
+            for t in range(PACK):
+                nc.tensor.transpose(rb_rows[a][:, t, :], rb_sb[:, a, t : t + 1].to_broadcast([P, P]), ident[:])
+
+        def gather(engine, dst, table, offsets, piece):
+            window = table[:].indirect(offsets[:, piece * PIECE // 16 : (piece + 1) * PIECE // 16])
+            if engine == "v":
+                nc.vector.tensor_copy(dst, window)
+            else:
+                nc.scalar.activation(dst, window, COPY)
+
+        def gather_x(h, engines):
+            for piece, engine in enumerate(engines):
+                gather(engine, x_picked[h][:, PAD + piece * PIECE : PAD + (piece + 1) * PIECE], x_table[h], list_x, piece)
+
+        g_picked = {}
+
+        def gather_g(h, first, engines, tag):
+            picked = keep.tile([P, PIECE * len(engines)], F32, name="g_picked%d%d" % (h, first), tag=tag, align_bytes=64)
+            for i, engine in enumerate(engines):
+                gather(engine, picked[:, i * PIECE : (i + 1) * PIECE], g_table[h], list_g, first + i)
+            g_picked[h, first] = picked
+
+        grouped = {}
+        turned = {}
+        codes = {}
+        scales = {}
+
+        def step_x(h, a, bank, tag):
+            steps = keep.tile([P, J_PASS], F32, name="steps%d%d" % (h, a), tag=tag, align_bytes=64)
+            j0 = PAD + a * J_PASS
+            nc.vector.scalar_tensor_tensor(
+                out=steps[:], in0=x_picked[h][:, j0 - 1 : j0 - 1 + J_PASS], scalar=-0.6,
+                in1=x_picked[h][:, j0 : j0 + J_PASS], op0=MULT, op1=ADD)
+            ps = psum.tile([P, PACK, P], F32, name="turned_x%d%d" % (h, a), tag="bank%d" % bank)
+            for t in range(PACK):
+                nc.tensor.transpose(ps[:, t, :], steps[:, t:J_PASS:PACK], ident[:])
+            turned["x", h, a] = ps
+
+        def weigh_x(h, a, tag):
+            g = keep.tile([P, P, PACK], BF16, name="grouped_x%d%d" % (h, a), tag=tag, align_bytes=64)
+            nc.vector.tensor_tensor(
+                out=g[:], in0=turned["x", h, a][:].rearrange("p t r -> p r t"),
+                in1=ra_sb[:, a, :].unsqueeze(1).to_broadcast([P, P, PACK]), op=MULT)
+            grouped["x", h, a] = g
+
+        def bound_g(h, a, bank, tag, firsts):
+            bounded = keep.tile([P, J_PASS], BF16, name="bounded%d%d" % (h, a), tag=tag, align_bytes=64)
+            for first in firsts:
+                picked = g_picked[h, first]
+                width = picked.shape[1]
+                c0 = first * PIECE - a * J_PASS
+                nc.vector.scalar_tensor_tensor(
+                    out=bounded[:, c0 : c0 + width].rearrange("p (q t) -> p q t", t=PACK),
+                    in0=picked[:].rearrange("p (q t) -> p q t", t=PACK),
+                    scalar=cp_sb[:, h : h + 1],
+                    in1=rb_rows[a][:, :, c0 // PACK : (c0 + width) // PACK].rearrange("p t q -> p q t"), op0=MIN, op1=MULT)
+            words = bounded[:].bitcast(F32)
+            ps = psum.tile([P, 2, P], F32, name="turned_g%d%d" % (h, a), tag="bank%d" % bank)
+            for u in range(2):
+                nc.tensor.transpose(ps[:, u, :], words[:, u : J_PASS // 2 : 2], ident[:])
+            turned["g", h, a] = ps
+
+        def weave_g(h, a, engine):
+            g = keep.tile([P, P * PACK], BF16, name="grouped_g%d%d" % (h, a), align_bytes=64)
+            dst = g[:].bitcast(F32).rearrange("p (r u) -> p r u", u=2)
+            src = turned["g", h, a][:].rearrange("p u r -> p r u")
+            if engine == "v":
+                nc.vector.tensor_copy(dst, src)
+            else:
+                nc.scalar.copy(dst, src)
+            grouped["g", h, a] = g
+
+        def quantize(side, h, a, tag=""):
+            c = keep.tile([P, P], U32, name="codes_%s%d%d" % (side, h, a), tag=tag, align_bytes=64)
+            s = keep.tile([P, P], U8, name="scales_%s%d%d" % (side, h, a), align_bytes=64)
+            src = grouped[side, h, a][:]
+            if side == "x":
+                src = src.rearrange("p r t -> p (r t)")
+            nc.vector.quantize_mx(out=c[:].bitcast(E5M2X4), scales=s[:], in_=src)
+            codes[side, h, a] = c
+            scales[side, h, a] = s
+
+        def multiply(acc, kh, nh, a):
+            nc.tensor.matmul_mx(
+                out=acc, lhsT=codes["x", kh, a][:].bitcast(E5M2X4), lhsT_scale=scales["x", kh, a][:],
+                rhs=codes["g", nh, a][:].bitcast(E5M2X4), rhs_scale=scales["g", nh, a][:],
+                start=(a == 0), stop=(a == PASSES - 1))
+
+        gather_x(0, "svss")
+        step_x(0, 0, 2, "steps00")
+        step_x(0, 1, 3, "steps01")
+        gather_x(1, "ssss")
+        weigh_x(0, 0, "A")
+        quantize("x", 0, 0)
+        weigh_x(0, 1, "B")
+        step_x(1, 0, 4, "A")
+        quantize("x", 0, 1)
+        step_x(1, 1, 5, "B")
+        gather_g(0, 0, "ss", "g00")
+        gather_g(0, 2, "ss", "g02")
+        gather_g(1, 0, "ss", "E")
+        gather_g(1, 2, "s", "F")
+        weigh_x(1, 0, "C")
+        bound_g(0, 0, 2, "A", [0])
+        weigh_x(1, 1, "D")
+        quantize("x", 1, 0)
+        quantize("x", 1, 1)
+        bound_g(0, 1, 3, "B", [2])
+        gather_g(1, 3, "v", "C")
+        bound_g(1, 0, 4, "D", [0])
+        bound_g(1, 1, 5, "B", [2, 3])
+        weave_g(0, 0, "s")
+        weave_g(0, 1, "s")
+        quantize("g", 0, 0, "E")
+        quantize("g", 0, 1, "F")
+        w_sb = keep.tile([P, 2, N], F32, name="w_sb")
+        w_first = psum.tile([P, 2, P], F32, name="w_first", tag="bank6")
+        for kh in range(2):
+            for a in range(PASSES):
+                multiply(w_first[:, kh, :], kh, 0, a)
+        weave_g(1, 0, "s")
+        weave_g(1, 1, "s")
+        nc.scalar.copy(w_sb[:, :, 0:P], w_first[:])
+        quantize("g", 1, 0)
+        quantize("g", 1, 1)
+        w_last = [psum.tile([P, P], F32, name="w_last%d" % kh, tag="bank%d" % (7, 2)[kh]) for kh in range(2)]
+        for a in range(PASSES):
+            for kh in range(2):
+                multiply(w_last[kh][:], kh, 1, a)
+        nc.vector.tensor_copy(w_sb[:, 0, P:N], w_last[0][:])
+        nc.scalar.copy(w_sb[:, 1, P:N], w_last[1][:])
+        picked_w = [keep.tile([P, E], F32, name="picked_w%d" % kh) for kh in range(2)]
+        nc.vector.tensor_copy(picked_w[0][:], w_sb[:, 0, :].indirect(list_w[:]))
+        nc.scalar.activation(picked_w[1][:], w_sb[:, 1, :].indirect(list_w[:]), COPY)
+        for kh in range(2):
+            result = keep.tile([P, E], F32, name="result%d" % kh)
+            nc.vector.scalar_tensor_tensor(
+                out=result[:], in0=picked_w[kh][:], scalar=0.04, in1=old_sb[:, kh, :], op0=MULT, op1=ADD)
+            nc.sync.dma_start(out[kh * P : (kh + 1) * P, :], result[:])

@@ -1,7 +1,6 @@
 from contextlib import ExitStack
 
 import concourse.mybir as mybir
-from concourse.masks import make_identity
 
 K, J, N, T, V, E = 256, 1024, 256, 2048, 2048, 128
 FLOPS = 2 * J * K * N
@@ -21,8 +20,10 @@ P = 128
 PACK = 4
 J_PASS = P * PACK
 PASSES = J // J_PASS
-PIECE = 256
+LAST = 128
 PAD = 8
+RB_ROWS = J // P
+QUAD = 32
 
 
 def tile_list_moment_steps_bounded_columns_kernel(tc, xf, ra, gt, rb, cp, old, offs, offs2, offs3, out):
@@ -30,6 +31,7 @@ def tile_list_moment_steps_bounded_columns_kernel(tc, xf, ra, gt, rb, cp, old, o
     with ExitStack() as ctx:
         lists = ctx.enter_context(tc.tile_pool(name="lists", bufs=1))
         keep = ctx.enter_context(tc.tile_pool(name="keep", bufs=1))
+        staged = ctx.enter_context(tc.tile_pool(name="staged", bufs=2))
         psum = ctx.enter_context(tc.psum_pool(name="psum", bufs=1))
 
         list_x = lists.tile([P, J // 16], U16, name="list_x")
@@ -37,21 +39,20 @@ def tile_list_moment_steps_bounded_columns_kernel(tc, xf, ra, gt, rb, cp, old, o
         list_w = lists.tile([P, E // 16], U16, name="list_w")
         x_table = [keep.tile([P, T], F32, name="x_table%d" % h) for h in range(2)]
         g_table = [keep.tile([P, V], F32, name="g_table%d" % h) for h in range(2)]
-        ra_sb = keep.tile([P, PASSES, PACK], F32, name="ra_sb")
-        rb_sb = keep.tile([P, PASSES, PACK], F32, name="rb_sb")
-        cp_sb = keep.tile([P, 2], F32, name="cp_sb")
+        ra_sb = keep.tile([P, PASSES, PAD], F32, name="ra_sb")
+        rows = keep.tile([P, P], F32, name="rows")
+        columns = keep.tile([P, RB_ROWS + 2], F32, name="columns")
         old_sb = keep.tile([P, 2, E], F32, name="old_sb")
         ident = keep.tile([P, P], F32, name="ident")
 
         zero = keep.tile([P, 1], F32, name="zero")
+        nc.vector.memset(rows[:], 0.0)
         nc.vector.memset(zero[:], 0.0)
-        make_identity(nc, ident[:])
         nc.sync.dma_start(list_x[:], offs)
-        nc.scalar.dma_start(ra_sb[:], ra[0, :].rearrange("(a q t) -> q a t", a=PASSES, t=PACK))
+        nc.scalar.dma_start(ra_sb[:, :, 0:PACK], ra[0, :].rearrange("(a q t) -> q a t", a=PASSES, t=PACK))
+        nc.scalar.dma_start(rows[0:RB_ROWS, :], rb[0, :].rearrange("(m n) -> m n", n=P))
+        nc.scalar.dma_start(rows[RB_ROWS : RB_ROWS + 2, :], cp.rearrange("(h p) o -> h (p o)", p=P))
         nc.sync.dma_start(x_table[0][:], xf[0:P, :])
-        nc.scalar.dma_start(rb_sb[:], rb[0, :].rearrange("(a q t) -> q a t", a=PASSES, t=PACK))
-        with nc.allow_non_contiguous_dma(reason="one bound a partition"):
-            nc.scalar.dma_start(cp_sb[:], cp.rearrange("(h p) o -> p (h o)", p=P))
         nc.sync.dma_start(x_table[1][:], xf[P : 2 * P, :])
         nc.sync.dma_start(list_g[:], offs2)
         nc.sync.dma_start(g_table[0][:], gt[0:P, :])
@@ -63,37 +64,50 @@ def tile_list_moment_steps_bounded_columns_kernel(tc, xf, ra, gt, rb, cp, old, o
         for h in range(2):
             nc.scalar.activation(x_picked[h][:, PAD - 1 : PAD], zero[:], COPY)
 
-        rb_rows = [psum.tile([P, PACK, P], F32, name="rb_rows%d" % a, tag="bank%d" % a) for a in range(PASSES)]
-        for a in range(PASSES):
-            for t in range(PACK):
-                nc.tensor.transpose(rb_rows[a][:, t, :], rb_sb[:, a, t : t + 1].to_broadcast([P, P]), ident[:])
+        ones = keep.tile([P, QUAD], F32, name="ones")
+        count_along = keep.tile([P, QUAD], F32, name="count_along", align_bytes=64)
+        count_down = keep.tile([P, QUAD], F32, name="count_down", align_bytes=64)
+        nc.vector.memset(ones[:], 1.0)
+        nc.vector.memset(ident[:], 0.0)
+        nc.vector.tensor_tensor_scan(count_along[:], ones[:], ones[:], 0.0, MULT, ADD)
+        nc.vector.transpose(count_down[:], count_along[:])
+        for q0 in range(0, P, QUAD):
+            nc.vector.tensor_tensor(
+                ident[q0 : q0 + QUAD, q0 : q0 + QUAD], count_along[q0 : q0 + QUAD, :], count_down[q0 : q0 + QUAD, :],
+                mybir.AluOpType.is_equal)
 
-        def gather(engine, dst, table, offsets, piece):
-            window = table[:].indirect(offsets[:, piece * PIECE // 16 : (piece + 1) * PIECE // 16])
+        turned_rows = psum.tile([P, P], F32, name="turned_rows", tag="bank7")
+        nc.tensor.transpose(turned_rows[:], rows[:], ident[:])
+        nc.vector.tensor_copy(columns[:], turned_rows[:, 0 : RB_ROWS + 2])
+        rb_rows = [psum.tile([P, J_PASS], F32, name="rb_rows%d" % a, tag="bank%d" % a) for a in range(PASSES)]
+        for m in range(RB_ROWS):
+            a, c = divmod(m * P, J_PASS)
+            nc.tensor.transpose(rb_rows[a][:, c : c + P], columns[:, m : m + 1].to_broadcast([P, P]), ident[:])
+
+        def gather(engine, dst, table, offsets, first, count):
+            window = table[:].indirect(offsets[:, first // 16 : (first + count) // 16])
             if engine == "v":
                 nc.vector.tensor_copy(dst, window)
             else:
                 nc.scalar.activation(dst, window, COPY)
 
-        def gather_x(h, engines):
-            for piece, engine in enumerate(engines):
-                gather(engine, x_picked[h][:, PAD + piece * PIECE : PAD + (piece + 1) * PIECE], x_table[h], list_x, piece)
+        def gather_x(h, first, count, engine):
+            gather(engine, x_picked[h][:, PAD + first : PAD + first + count], x_table[h], list_x, first, count)
 
         g_picked = {}
 
-        def gather_g(h, first, engines, tag):
-            picked = keep.tile([P, PIECE * len(engines)], F32, name="g_picked%d%d" % (h, first), tag=tag, align_bytes=64)
-            for i, engine in enumerate(engines):
-                gather(engine, picked[:, i * PIECE : (i + 1) * PIECE], g_table[h], list_g, first + i)
+        def gather_g(h, first, count, tag=""):
+            picked = keep.tile([P, count], F32, name="g_picked%d_%d" % (h, first), tag=tag, align_bytes=64)
+            gather("s", picked[:], g_table[h], list_g, first, count)
             g_picked[h, first] = picked
 
-        grouped = {}
         turned = {}
+        grouped = {}
         codes = {}
         scales = {}
 
-        def step_x(h, a, bank, tag):
-            steps = keep.tile([P, J_PASS], F32, name="steps%d%d" % (h, a), tag=tag, align_bytes=64)
+        def step_x(h, a, bank):
+            steps = staged.tile([P, J_PASS], F32, name="steps%d%d" % (h, a), tag="staged", align_bytes=64)
             j0 = PAD + a * J_PASS
             nc.vector.scalar_tensor_tensor(
                 out=steps[:], in0=x_picked[h][:, j0 - 1 : j0 - 1 + J_PASS], scalar=-0.6,
@@ -103,104 +117,100 @@ def tile_list_moment_steps_bounded_columns_kernel(tc, xf, ra, gt, rb, cp, old, o
                 nc.tensor.transpose(ps[:, t, :], steps[:, t:J_PASS:PACK], ident[:])
             turned["x", h, a] = ps
 
-        def weigh_x(h, a, tag):
-            g = keep.tile([P, P, PACK], BF16, name="grouped_x%d%d" % (h, a), tag=tag, align_bytes=64)
+        def weigh_x(h, a):
             nc.vector.tensor_tensor(
-                out=g[:], in0=turned["x", h, a][:].rearrange("p t r -> p r t"),
-                in1=ra_sb[:, a, :].unsqueeze(1).to_broadcast([P, P, PACK]), op=MULT)
-            grouped["x", h, a] = g
+                out=grouped["x", h][:, a * J_PASS : (a + 1) * J_PASS].rearrange("p (r t) -> p r t", t=PACK),
+                in0=turned["x", h, a][:].rearrange("p t r -> p r t"),
+                in1=ra_sb[:, a, 0:PACK].unsqueeze(1).to_broadcast([P, P, PACK]), op=MULT)
 
-        def bound_g(h, a, bank, tag, firsts):
-            bounded = keep.tile([P, J_PASS], BF16, name="bounded%d%d" % (h, a), tag=tag, align_bytes=64)
+        def bound_g(h, a, bank, firsts):
+            bounded = staged.tile([P, J_PASS], BF16, name="bounded%d%d" % (h, a), tag="staged", align_bytes=64)
             for first in firsts:
                 picked = g_picked[h, first]
                 width = picked.shape[1]
-                c0 = first * PIECE - a * J_PASS
+                c0 = first - a * J_PASS
                 nc.vector.scalar_tensor_tensor(
-                    out=bounded[:, c0 : c0 + width].rearrange("p (q t) -> p q t", t=PACK),
-                    in0=picked[:].rearrange("p (q t) -> p q t", t=PACK),
-                    scalar=cp_sb[:, h : h + 1],
-                    in1=rb_rows[a][:, :, c0 // PACK : (c0 + width) // PACK].rearrange("p t q -> p q t"), op0=MIN, op1=MULT)
+                    out=bounded[:, c0 : c0 + width], in0=picked[:],
+                    scalar=columns[:, RB_ROWS + h : RB_ROWS + h + 1],
+                    in1=rb_rows[a][:, c0 : c0 + width], op0=MIN, op1=MULT)
             words = bounded[:].bitcast(F32)
             ps = psum.tile([P, 2, P], F32, name="turned_g%d%d" % (h, a), tag="bank%d" % bank)
             for u in range(2):
                 nc.tensor.transpose(ps[:, u, :], words[:, u : J_PASS // 2 : 2], ident[:])
             turned["g", h, a] = ps
 
-        def weave_g(h, a, engine):
-            g = keep.tile([P, P * PACK], BF16, name="grouped_g%d%d" % (h, a), align_bytes=64)
-            dst = g[:].bitcast(F32).rearrange("p (r u) -> p r u", u=2)
-            src = turned["g", h, a][:].rearrange("p u r -> p r u")
-            if engine == "v":
-                nc.vector.tensor_copy(dst, src)
-            else:
-                nc.scalar.copy(dst, src)
-            grouped["g", h, a] = g
+        def weave_g(h, a):
+            dst = grouped["g", h][:, a * J_PASS : (a + 1) * J_PASS].bitcast(F32).rearrange("p (r u) -> p r u", u=2)
+            nc.scalar.copy(dst, turned["g", h, a][:].rearrange("p u r -> p r u"))
 
-        def quantize(side, h, a, tag=""):
-            c = keep.tile([P, P], U32, name="codes_%s%d%d" % (side, h, a), tag=tag, align_bytes=64)
-            s = keep.tile([P, P], U8, name="scales_%s%d%d" % (side, h, a), align_bytes=64)
-            src = grouped[side, h, a][:]
-            if side == "x":
-                src = src.rearrange("p r t -> p (r t)")
-            nc.vector.quantize_mx(out=c[:].bitcast(E5M2X4), scales=s[:], in_=src)
-            codes[side, h, a] = c
-            scales[side, h, a] = s
+        def quantize(side, h, a0, a1):
+            nc.vector.quantize_mx(
+                out=codes[side, h][:, a0 * P : a1 * P].bitcast(E5M2X4), scales=scales[side, h][:, a0 * P : a1 * P],
+                in_=grouped[side, h][:, a0 * J_PASS : a1 * J_PASS])
 
         def multiply(acc, kh, nh, a):
+            cols = slice(a * P, (a + 1) * P)
             nc.tensor.matmul_mx(
-                out=acc, lhsT=codes["x", kh, a][:].bitcast(E5M2X4), lhsT_scale=scales["x", kh, a][:],
-                rhs=codes["g", nh, a][:].bitcast(E5M2X4), rhs_scale=scales["g", nh, a][:],
+                out=acc, lhsT=codes["x", kh][:, cols].bitcast(E5M2X4), lhsT_scale=scales["x", kh][:, cols],
+                rhs=codes["g", nh][:, cols].bitcast(E5M2X4), rhs_scale=scales["g", nh][:, cols],
                 start=(a == 0), stop=(a == PASSES - 1))
 
-        gather_x(0, "svss")
-        step_x(0, 0, 2, "steps00")
-        step_x(0, 1, 3, "steps01")
-        gather_x(1, "ssss")
-        weigh_x(0, 0, "A")
-        quantize("x", 0, 0)
-        weigh_x(0, 1, "B")
-        step_x(1, 0, 4, "A")
-        quantize("x", 0, 1)
-        step_x(1, 1, 5, "B")
-        gather_g(0, 0, "ss", "g00")
-        gather_g(0, 2, "ss", "g02")
-        gather_g(1, 0, "ss", "E")
-        gather_g(1, 2, "s", "F")
-        weigh_x(1, 0, "C")
-        bound_g(0, 0, 2, "A", [0])
-        weigh_x(1, 1, "D")
-        quantize("x", 1, 0)
-        quantize("x", 1, 1)
-        bound_g(0, 1, 3, "B", [2])
-        gather_g(1, 3, "v", "C")
-        bound_g(1, 0, 4, "D", [0])
-        bound_g(1, 1, 5, "B", [2, 3])
-        weave_g(0, 0, "s")
-        weave_g(0, 1, "s")
-        quantize("g", 0, 0, "E")
-        quantize("g", 0, 1, "F")
+        for side in "xg":
+            for h in range(2):
+                codes[side, h] = keep.tile([P, PASSES * P], U32, name="codes_%s%d" % (side, h), align_bytes=64)
+                scales[side, h] = keep.tile([P, PASSES * P], U8, name="scales_%s%d" % (side, h), align_bytes=64)
+        for key in (("x", 0), ("x", 1), ("g", 1)):
+            grouped[key] = keep.tile([P, J], BF16, name="grouped_%s%d" % key, align_bytes=64)
+
+        gather_x(0, 0, 256, "s")
+        gather_x(0, 256, 256, "v")
+        gather_x(0, 512, 512, "s")
+        for a in range(PASSES):
+            gather_x(1, a * J_PASS, J_PASS, "s")
+        for a in range(PASSES):
+            gather_g(0, a * J_PASS, J_PASS)
+        gather_g(1, 0, J_PASS, "held")
+        gather_g(1, J_PASS, J_PASS - LAST)
+        gather_g(1, J - LAST, LAST)
+        step_x(0, 0, 2)
+        step_x(0, 1, 3)
+        weigh_x(0, 0)
+        step_x(1, 0, 4)
+        weigh_x(0, 1)
+        step_x(1, 1, 5)
+        quantize("x", 0, 0, 2)
+        weigh_x(1, 0)
+        bound_g(0, 0, 2, [0])
+        weigh_x(1, 1)
+        bound_g(0, 1, 3, [J_PASS])
+        quantize("x", 1, 0, 2)
+        bound_g(1, 0, 4, [0])
+        bound_g(1, 1, 5, [J_PASS, J - LAST])
+        grouped["g", 0] = keep.tile([P, J], BF16, name="grouped_g0", tag="held", align_bytes=64)
+        weave_g(0, 0)
+        weave_g(0, 1)
+        quantize("g", 0, 0, 2)
         w_sb = keep.tile([P, 2, N], F32, name="w_sb")
         w_first = psum.tile([P, 2, P], F32, name="w_first", tag="bank6")
         for kh in range(2):
             for a in range(PASSES):
                 multiply(w_first[:, kh, :], kh, 0, a)
-        weave_g(1, 0, "s")
-        weave_g(1, 1, "s")
+        weave_g(1, 0)
+        weave_g(1, 1)
         nc.scalar.copy(w_sb[:, :, 0:P], w_first[:])
-        quantize("g", 1, 0)
-        quantize("g", 1, 1)
+        quantize("g", 1, 0, 1)
+        quantize("g", 1, 1, 2)
         w_last = [psum.tile([P, P], F32, name="w_last%d" % kh, tag="bank%d" % (7, 2)[kh]) for kh in range(2)]
         for a in range(PASSES):
             for kh in range(2):
                 multiply(w_last[kh][:], kh, 1, a)
-        nc.vector.tensor_copy(w_sb[:, 0, P:N], w_last[0][:])
-        nc.scalar.copy(w_sb[:, 1, P:N], w_last[1][:])
+        nc.scalar.copy(w_sb[:, 0, P:N], w_last[0][:])
+        nc.vector.tensor_copy(w_sb[:, 1, P:N], w_last[1][:])
         picked_w = [keep.tile([P, E], F32, name="picked_w%d" % kh) for kh in range(2)]
         nc.vector.tensor_copy(picked_w[0][:], w_sb[:, 0, :].indirect(list_w[:]))
         nc.scalar.activation(picked_w[1][:], w_sb[:, 1, :].indirect(list_w[:]), COPY)
-        for kh in range(2):
+        for kh, queue in ((1, nc.sync), (0, nc.scalar)):
             result = keep.tile([P, E], F32, name="result%d" % kh)
             nc.vector.scalar_tensor_tensor(
                 out=result[:], in0=picked_w[kh][:], scalar=0.04, in1=old_sb[:, kh, :], op0=MULT, op1=ADD)
-            nc.sync.dma_start(out[kh * P : (kh + 1) * P, :], result[:])
+            queue.dma_start(out[kh * P : (kh + 1) * P, :], result[:])

@@ -1,6 +1,7 @@
 from contextlib import ExitStack
 
 import concourse.mybir as mybir
+from concourse.masks import make_identity
 
 K, J, N, T, V, E = 256, 1024, 256, 2048, 2048, 128
 FLOPS = 2 * J * K * N
@@ -23,7 +24,6 @@ PASSES = J // J_PASS
 LAST = 128
 PAD = 8
 RB_ROWS = J // P
-QUAD = 32
 
 
 def tile_list_moment_steps_bounded_columns_kernel(tc, xf, ra, gt, rb, cp, old, offs, offs2, offs3, out):
@@ -48,12 +48,13 @@ def tile_list_moment_steps_bounded_columns_kernel(tc, xf, ra, gt, rb, cp, old, o
         zero = keep.tile([P, 1], F32, name="zero")
         nc.vector.memset(rows[:], 0.0)
         nc.vector.memset(zero[:], 0.0)
+        make_identity(nc, ident[:])
         nc.sync.dma_start(list_x[:], offs)
-        nc.scalar.dma_start(ra_sb[:, :, 0:PACK], ra[0, :].rearrange("(a q t) -> q a t", a=PASSES, t=PACK))
-        nc.scalar.dma_start(rows[0:RB_ROWS, :], rb[0, :].rearrange("(m n) -> m n", n=P))
-        nc.scalar.dma_start(rows[RB_ROWS : RB_ROWS + 2, :], cp.rearrange("(h p) o -> h (p o)", p=P))
         nc.sync.dma_start(x_table[0][:], xf[0:P, :])
+        nc.sync.dma_start(rows[0:RB_ROWS, :], rb[0, :].rearrange("(m n) -> m n", n=P))
+        nc.sync.dma_start(rows[RB_ROWS : RB_ROWS + 2, :], cp.rearrange("(h p) o -> h (p o)", p=P))
         nc.sync.dma_start(x_table[1][:], xf[P : 2 * P, :])
+        nc.sync.dma_start(ra_sb[:, :, 0:PACK], ra[0, :].rearrange("(a q t) -> q a t", a=PASSES, t=PACK))
         nc.sync.dma_start(list_g[:], offs2)
         nc.sync.dma_start(g_table[0][:], gt[0:P, :])
         nc.sync.dma_start(g_table[1][:], gt[P : 2 * P, :])
@@ -64,25 +65,15 @@ def tile_list_moment_steps_bounded_columns_kernel(tc, xf, ra, gt, rb, cp, old, o
         for h in range(2):
             nc.scalar.activation(x_picked[h][:, PAD - 1 : PAD], zero[:], COPY)
 
-        ones = keep.tile([P, QUAD], F32, name="ones")
-        count_along = keep.tile([P, QUAD], F32, name="count_along", align_bytes=64)
-        count_down = keep.tile([P, QUAD], F32, name="count_down", align_bytes=64)
-        nc.vector.memset(ones[:], 1.0)
-        nc.vector.memset(ident[:], 0.0)
-        nc.vector.tensor_tensor_scan(count_along[:], ones[:], ones[:], 0.0, MULT, ADD)
-        nc.vector.transpose(count_down[:], count_along[:])
-        for q0 in range(0, P, QUAD):
-            nc.vector.tensor_tensor(
-                ident[q0 : q0 + QUAD, q0 : q0 + QUAD], count_along[q0 : q0 + QUAD, :], count_down[q0 : q0 + QUAD, :],
-                mybir.AluOpType.is_equal)
-
         turned_rows = psum.tile([P, P], F32, name="turned_rows", tag="bank7")
         nc.tensor.transpose(turned_rows[:], rows[:], ident[:])
-        nc.vector.tensor_copy(columns[:], turned_rows[:, 0 : RB_ROWS + 2])
-        rb_rows = [psum.tile([P, J_PASS], F32, name="rb_rows%d" % a, tag="bank%d" % a) for a in range(PASSES)]
-        for m in range(RB_ROWS):
-            a, c = divmod(m * P, J_PASS)
-            nc.tensor.transpose(rb_rows[a][:, c : c + P], columns[:, m : m + 1].to_broadcast([P, P]), ident[:])
+        rb_rows = {}
+
+        def spread_rb(a, bank):
+            rb_rows[a] = psum.tile([P, J_PASS], F32, name="rb_rows%d" % a, tag="bank%d" % bank)
+            for c in range(PACK):
+                m = a * PACK + c
+                nc.tensor.transpose(rb_rows[a][:, c * P : (c + 1) * P], columns[:, m : m + 1].to_broadcast([P, P]), ident[:])
 
         def gather(engine, dst, table, offsets, first, count):
             window = table[:].indirect(offsets[:, first // 16 : (first + count) // 16])
@@ -124,7 +115,7 @@ def tile_list_moment_steps_bounded_columns_kernel(tc, xf, ra, gt, rb, cp, old, o
                 in1=ra_sb[:, a, 0:PACK].unsqueeze(1).to_broadcast([P, P, PACK]), op=MULT)
 
         def bound_g(h, a, bank, firsts):
-            bounded = staged.tile([P, J_PASS], BF16, name="bounded%d%d" % (h, a), tag="staged", align_bytes=64)
+            bounded = keep.tile([P, J_PASS], BF16, name="bounded%d%d" % (h, a), align_bytes=64)
             for first in firsts:
                 picked = g_picked[h, first]
                 width = picked.shape[1]
@@ -157,36 +148,42 @@ def tile_list_moment_steps_bounded_columns_kernel(tc, xf, ra, gt, rb, cp, old, o
 
         for side in "xg":
             for h in range(2):
-                codes[side, h] = keep.tile([P, PASSES * P], U32, name="codes_%s%d" % (side, h), align_bytes=64)
                 scales[side, h] = keep.tile([P, PASSES * P], U8, name="scales_%s%d" % (side, h), align_bytes=64)
+        for key in (("x", 0), ("g", 0), ("g", 1)):
+            codes[key] = keep.tile([P, PASSES * P], U32, name="codes_%s%d" % key, align_bytes=64)
         for key in (("x", 0), ("x", 1), ("g", 1)):
             grouped[key] = keep.tile([P, J], BF16, name="grouped_%s%d" % key, align_bytes=64)
 
         gather_x(0, 0, 256, "s")
         gather_x(0, 256, 256, "v")
         gather_x(0, 512, 512, "s")
-        for a in range(PASSES):
-            gather_x(1, a * J_PASS, J_PASS, "s")
-        for a in range(PASSES):
-            gather_g(0, a * J_PASS, J_PASS)
-        gather_g(1, 0, J_PASS, "held")
-        gather_g(1, J_PASS, J_PASS - LAST)
-        gather_g(1, J - LAST, LAST)
         step_x(0, 0, 2)
         step_x(0, 1, 3)
-        weigh_x(0, 0)
+        nc.vector.tensor_copy(columns[:], turned_rows[:, 0 : RB_ROWS + 2])
+        spread_rb(0, 0)
+        gather_x(1, 0, 256, "s")
+        gather_x(1, 256, 256, "v")
+        gather_x(1, 512, 512, "s")
+        for a in range(PASSES):
+            gather_g(0, a * J_PASS, J_PASS)
+        gather_g(1, 0, J_PASS, "held_a")
+        gather_g(1, J_PASS, J_PASS - LAST, "held_b")
+        gather_g(1, J - LAST, LAST)
         step_x(1, 0, 4)
-        weigh_x(0, 1)
+        weigh_x(0, 0)
         step_x(1, 1, 5)
-        quantize("x", 0, 0, 2)
+        weigh_x(0, 1)
         weigh_x(1, 0)
-        bound_g(0, 0, 2, [0])
+        quantize("x", 0, 0, 2)
+        spread_rb(1, 4)
         weigh_x(1, 1)
+        bound_g(0, 0, 2, [0])
         bound_g(0, 1, 3, [J_PASS])
-        quantize("x", 1, 0, 2)
-        bound_g(1, 0, 4, [0])
+        bound_g(1, 0, 1, [0])
         bound_g(1, 1, 5, [J_PASS, J - LAST])
-        grouped["g", 0] = keep.tile([P, J], BF16, name="grouped_g0", tag="held", align_bytes=64)
+        codes["x", 1] = keep.tile([P, PASSES * P], U32, name="codes_x1", tag="held_b", align_bytes=64)
+        quantize("x", 1, 0, 2)
+        grouped["g", 0] = keep.tile([P, J], BF16, name="grouped_g0", tag="held_a", align_bytes=64)
         weave_g(0, 0)
         weave_g(0, 1)
         quantize("g", 0, 0, 2)

@@ -49,8 +49,8 @@ def tile_list_moment_steps_bounded_columns_kernel(tc, xf, ra, gt, rb, cp, old, o
         nc.vector.memset(rows[:], 0.0)
         nc.vector.memset(zero[:], 0.0)
         make_identity(nc, ident[:])
-        nc.sync.dma_start(list_x[:], offs)
         nc.sync.dma_start(x_table[0][:], xf[0:P, :])
+        nc.sync.dma_start(list_x[:], offs)
         nc.sync.dma_start(rows[0:RB_ROWS, :], rb[0, :].rearrange("(m n) -> m n", n=P))
         nc.sync.dma_start(rows[RB_ROWS : RB_ROWS + 2, :], cp.rearrange("(h p) o -> h (p o)", p=P))
         nc.sync.dma_start(x_table[1][:], xf[P : 2 * P, :])
@@ -101,11 +101,12 @@ def tile_list_moment_steps_bounded_columns_kernel(tc, xf, ra, gt, rb, cp, old, o
             steps = staged.tile([P, J_PASS], F32, name="steps%d%d" % (h, a), tag="staged", align_bytes=64)
             j0 = PAD + a * J_PASS
             nc.vector.scalar_tensor_tensor(
-                out=steps[:], in0=x_picked[h][:, j0 - 1 : j0 - 1 + J_PASS], scalar=-0.6,
-                in1=x_picked[h][:, j0 : j0 + J_PASS], op0=MULT, op1=ADD)
+                out=steps[:].rearrange("p (t q) -> p q t", t=PACK),
+                in0=x_picked[h][:, j0 - 1 : j0 - 1 + J_PASS].rearrange("p (q t) -> p q t", t=PACK), scalar=-0.6,
+                in1=x_picked[h][:, j0 : j0 + J_PASS].rearrange("p (q t) -> p q t", t=PACK), op0=MULT, op1=ADD)
             ps = psum.tile([P, PACK, P], F32, name="turned_x%d%d" % (h, a), tag="bank%d" % bank)
             for t in range(PACK):
-                nc.tensor.transpose(ps[:, t, :], steps[:, t:J_PASS:PACK], ident[:])
+                nc.tensor.transpose(ps[:, t, :], steps[:, t * P : (t + 1) * P], ident[:])
             turned["x", h, a] = ps
 
         def weigh_x(h, a):

from contextlib import ExitStack

import concourse.mybir as mybir
from concourse.masks import make_identity

K, J, N, T, V, E = 256, 1024, 256, 2048, 2048, 128
FLOPS = 2 * J * K * N

F32 = mybir.dt.float32
BF16 = mybir.dt.bfloat16
U32 = mybir.dt.uint32
U16 = mybir.dt.uint16
U8 = mybir.dt.uint8
E5M2X4 = mybir.dt.float8_e5m2_x4
MULT = mybir.AluOpType.mult
ADD = mybir.AluOpType.add
MIN = mybir.AluOpType.min
COPY = mybir.ActivationFunctionType.Copy

P = 128
PACK = 4
J_PASS = P * PACK
PASSES = J // J_PASS
LAST = 128
PAD = 8
RB_ROWS = J // P


def tile_list_moment_steps_bounded_columns_kernel(tc, xf, ra, gt, rb, cp, old, offs, offs2, offs3, out):
    nc = tc.nc
    with ExitStack() as ctx:
        lists = ctx.enter_context(tc.tile_pool(name="lists", bufs=1))
        keep = ctx.enter_context(tc.tile_pool(name="keep", bufs=1))
        staged = ctx.enter_context(tc.tile_pool(name="staged", bufs=2))
        psum = ctx.enter_context(tc.psum_pool(name="psum", bufs=1))

        list_x = lists.tile([P, J // 16], U16, name="list_x")
        list_g = lists.tile([P, J // 16], U16, name="list_g")
        list_w = lists.tile([P, E // 16], U16, name="list_w")
        x_table = [keep.tile([P, T], F32, name="x_table%d" % h) for h in range(2)]
        g_table = [keep.tile([P, V], F32, name="g_table%d" % h) for h in range(2)]
        ra_sb = keep.tile([P, PASSES, PAD], F32, name="ra_sb")
        rows = keep.tile([P, P], F32, name="rows")
        columns = keep.tile([P, RB_ROWS + 2], F32, name="columns")
        old_sb = keep.tile([P, 2, E], F32, name="old_sb")
        ident = keep.tile([P, P], F32, name="ident")

        zero = keep.tile([P, 1], F32, name="zero")
        nc.vector.memset(rows[:], 0.0)
        nc.vector.memset(zero[:], 0.0)
        make_identity(nc, ident[:])
        nc.sync.dma_start(x_table[0][:], xf[0:P, :])
        nc.sync.dma_start(list_x[:], offs)
        nc.sync.dma_start(rows[0:RB_ROWS, :], rb[0, :].rearrange("(m n) -> m n", n=P))
        nc.sync.dma_start(rows[RB_ROWS : RB_ROWS + 2, :], cp.rearrange("(h p) o -> h (p o)", p=P))
        nc.sync.dma_start(x_table[1][:], xf[P : 2 * P, :])
        nc.sync.dma_start(ra_sb[:, :, 0:PACK], ra[0, :].rearrange("(a q t) -> q a t", a=PASSES, t=PACK))
        nc.sync.dma_start(list_g[:], offs2)
        nc.sync.dma_start(g_table[0][:], gt[0:P, :])
        nc.sync.dma_start(g_table[1][:], gt[P : 2 * P, :])
        nc.sync.dma_start(list_w[:], offs3)
        nc.sync.dma_start(old_sb[:], old.rearrange("(h p) e -> p h e", p=P))

        x_picked = [keep.tile([P, PAD + J], F32, name="x_picked%d" % h) for h in range(2)]
        for h in range(2):
            nc.scalar.activation(x_picked[h][:, PAD - 1 : PAD], zero[:], COPY)

        turned_rows = psum.tile([P, P], F32, name="turned_rows", tag="bank7")
        nc.tensor.transpose(turned_rows[:], rows[:], ident[:])
        rb_rows = {}

        def spread_rb(a, bank):
            rb_rows[a] = psum.tile([P, J_PASS], F32, name="rb_rows%d" % a, tag="bank%d" % bank)
            for c in range(PACK):
                m = a * PACK + c
                nc.tensor.transpose(rb_rows[a][:, c * P : (c + 1) * P], columns[:, m : m + 1].to_broadcast([P, P]), ident[:])

        def gather(engine, dst, table, offsets, first, count):
            window = table[:].indirect(offsets[:, first // 16 : (first + count) // 16])
            if engine == "v":
                nc.vector.tensor_copy(dst, window)
            else:
                nc.scalar.activation(dst, window, COPY)

        def gather_x(h, first, count, engine):
            gather(engine, x_picked[h][:, PAD + first : PAD + first + count], x_table[h], list_x, first, count)

        g_picked = {}

        def gather_g(h, first, count, tag=""):
            picked = keep.tile([P, count], F32, name="g_picked%d_%d" % (h, first), tag=tag, align_bytes=64)
            gather("s", picked[:], g_table[h], list_g, first, count)
            g_picked[h, first] = picked

        turned = {}
        grouped = {}
        codes = {}
        scales = {}

        def step_x(h, a, bank):
            steps = staged.tile([P, J_PASS], F32, name="steps%d%d" % (h, a), tag="staged", align_bytes=64)
            j0 = PAD + a * J_PASS
            nc.vector.scalar_tensor_tensor(
                out=steps[:].rearrange("p (t q) -> p q t", t=PACK),
                in0=x_picked[h][:, j0 - 1 : j0 - 1 + J_PASS].rearrange("p (q t) -> p q t", t=PACK), scalar=-0.6,
                in1=x_picked[h][:, j0 : j0 + J_PASS].rearrange("p (q t) -> p q t", t=PACK), op0=MULT, op1=ADD)
            ps = psum.tile([P, PACK, P], F32, name="turned_x%d%d" % (h, a), tag="bank%d" % bank)
            for t in range(PACK):
                nc.tensor.transpose(ps[:, t, :], steps[:, t * P : (t + 1) * P], ident[:])
            turned["x", h, a] = ps

        def weigh_x(h, a):
            nc.vector.tensor_tensor(
                out=grouped["x", h][:, a * J_PASS : (a + 1) * J_PASS].rearrange("p (r t) -> p r t", t=PACK),
                in0=turned["x", h, a][:].rearrange("p t r -> p r t"),
                in1=ra_sb[:, a, 0:PACK].unsqueeze(1).to_broadcast([P, P, PACK]), op=MULT)

        def bound_g(h, a, bank, firsts):
            bounded = keep.tile([P, J_PASS], BF16, name="bounded%d%d" % (h, a), align_bytes=64)
            for first in firsts:
                picked = g_picked[h, first]
                width = picked.shape[1]
                c0 = first - a * J_PASS
                nc.vector.scalar_tensor_tensor(
                    out=bounded[:, c0 : c0 + width], in0=picked[:],
                    scalar=columns[:, RB_ROWS + h : RB_ROWS + h + 1],
                    in1=rb_rows[a][:, c0 : c0 + width], op0=MIN, op1=MULT)
            words = bounded[:].bitcast(F32)
            ps = psum.tile([P, 2, P], F32, name="turned_g%d%d" % (h, a), tag="bank%d" % bank)
            for u in range(2):
                nc.tensor.transpose(ps[:, u, :], words[:, u : J_PASS // 2 : 2], ident[:])
            turned["g", h, a] = ps

        def weave_g(h, a):
            dst = grouped["g", h][:, a * J_PASS : (a + 1) * J_PASS].bitcast(F32).rearrange("p (r u) -> p r u", u=2)
            nc.scalar.copy(dst, turned["g", h, a][:].rearrange("p u r -> p r u"))

        def quantize(side, h, a0, a1):
            nc.vector.quantize_mx(
                out=codes[side, h][:, a0 * P : a1 * P].bitcast(E5M2X4), scales=scales[side, h][:, a0 * P : a1 * P],
                in_=grouped[side, h][:, a0 * J_PASS : a1 * J_PASS])

        def multiply(acc, kh, nh, a):
            cols = slice(a * P, (a + 1) * P)
            nc.tensor.matmul_mx(
                out=acc, lhsT=codes["x", kh][:, cols].bitcast(E5M2X4), lhsT_scale=scales["x", kh][:, cols],
                rhs=codes["g", nh][:, cols].bitcast(E5M2X4), rhs_scale=scales["g", nh][:, cols],
                start=(a == 0), stop=(a == PASSES - 1))

        for side in "xg":
            for h in range(2):
                scales[side, h] = keep.tile([P, PASSES * P], U8, name="scales_%s%d" % (side, h), align_bytes=64)
        for key in (("x", 0), ("g", 0), ("g", 1)):
            codes[key] = keep.tile([P, PASSES * P], U32, name="codes_%s%d" % key, align_bytes=64)
        for key in (("x", 0), ("x", 1), ("g", 1)):
            grouped[key] = keep.tile([P, J], BF16, name="grouped_%s%d" % key, align_bytes=64)

        gather_x(0, 0, 256, "s")
        gather_x(0, 256, 256, "v")
        gather_x(0, 512, 512, "s")
        step_x(0, 0, 2)
        step_x(0, 1, 3)
        nc.vector.tensor_copy(columns[:], turned_rows[:, 0 : RB_ROWS + 2])
        spread_rb(0, 0)
        gather_x(1, 0, 256, "s")
        gather_x(1, 256, 256, "v")
        gather_x(1, 512, 512, "s")
        for a in range(PASSES):
            gather_g(0, a * J_PASS, J_PASS)
        gather_g(1, 0, J_PASS, "held_a")
        gather_g(1, J_PASS, J_PASS - LAST, "held_b")
        gather_g(1, J - LAST, LAST)
        step_x(1, 0, 4)
        weigh_x(0, 0)
        step_x(1, 1, 5)
        weigh_x(0, 1)
        weigh_x(1, 0)
        quantize("x", 0, 0, 2)
        spread_rb(1, 4)
        weigh_x(1, 1)
        bound_g(0, 0, 2, [0])
        bound_g(0, 1, 3, [J_PASS])
        bound_g(1, 0, 1, [0])
        bound_g(1, 1, 5, [J_PASS, J - LAST])
        codes["x", 1] = keep.tile([P, PASSES * P], U32, name="codes_x1", tag="held_b", align_bytes=64)
        quantize("x", 1, 0, 2)
        grouped["g", 0] = keep.tile([P, J], BF16, name="grouped_g0", tag="held_a", align_bytes=64)
        weave_g(0, 0)
        weave_g(0, 1)
        quantize("g", 0, 0, 2)
        w_sb = keep.tile([P, 2, N], F32, name="w_sb")
        w_first = psum.tile([P, 2, P], F32, name="w_first", tag="bank6")
        for kh in range(2):
            for a in range(PASSES):
                multiply(w_first[:, kh, :], kh, 0, a)
        weave_g(1, 0)
        weave_g(1, 1)
        nc.scalar.copy(w_sb[:, :, 0:P], w_first[:])
        quantize("g", 1, 0, 1)
        quantize("g", 1, 1, 2)
        w_last = [psum.tile([P, P], F32, name="w_last%d" % kh, tag="bank%d" % (7, 2)[kh]) for kh in range(2)]
        for a in range(PASSES):
            for kh in range(2):
                multiply(w_last[kh][:], kh, 1, a)
        nc.scalar.copy(w_sb[:, 0, P:N], w_last[0][:])
        nc.vector.tensor_copy(w_sb[:, 1, P:N], w_last[1][:])
        picked_w = [keep.tile([P, E], F32, name="picked_w%d" % kh) for kh in range(2)]
        nc.vector.tensor_copy(picked_w[0][:], w_sb[:, 0, :].indirect(list_w[:]))
        nc.scalar.activation(picked_w[1][:], w_sb[:, 1, :].indirect(list_w[:]), COPY)
        for kh, queue in ((1, nc.sync), (0, nc.scalar)):
            result = keep.tile([P, E], F32, name="result%d" % kh)
            nc.vector.scalar_tensor_tensor(
                out=result[:], in0=picked_w[kh][:], scalar=0.04, in1=old_sb[:, kh, :], op0=MULT, op1=ADD)
            queue.dma_start(out[kh * P : (kh + 1) * P, :], result[:])
